import numpy as np
import ml_dtypes


def mxq(x, axis, fmt="e4m3"):
    dtype, down = {"e4m3": (ml_dtypes.float8_e4m3fn, 7), "e5m2": (ml_dtypes.float8_e5m2, 14)}[fmt]
    v = np.moveaxis(np.asarray(x, np.float32).astype(ml_dtypes.bfloat16).astype(np.float64), axis, -1)
    blocks = v.reshape(v.shape[:-1] + (-1, 32))
    amax = np.abs(blocks).max(-1, keepdims=True)
    byte = np.maximum(np.where(amax > 0, np.frexp(amax)[1] - 1 + 127, 0) - down, 1)
    scale = np.exp2(byte - 127.0)
    codes = (blocks / scale).astype(np.float32).astype(dtype).astype(np.float64)
    return np.moveaxis((codes * scale).reshape(v.shape), -1, axis)


WIDE = False


def mx_kscale(k):
    if not WIDE:
        return np.ones(k)
    levels = np.array([10, -10, 5, -5, 0])
    if k % 512:
        return np.exp2(np.random.permutation(np.resize(levels, k // 32))).repeat(32)
    a = np.empty((k // 512, 16))
    for p in range(k // 512):
        a[p, :8] = np.random.permutation(np.resize(levels, 8))
        for g in range(8):
            far = levels[np.abs(levels - a[p, g]) >= 10]
            a[p, g + 8] = far[np.random.randint(len(far))]
    return np.exp2(a.ravel()).repeat(32)


def f64(x):
    return np.asarray(x).astype(np.float64)


def striped(idx):
    return np.tile(idx.reshape(-1, 16).T, (8, 1)).astype(np.uint16)


def unstriped(offs):
    return offs[:16].T.reshape(-1).astype(np.int64)


E2M1 = np.array([0.0, 0.5, 1.0, 1.5, 2.0, 3.0, 4.0, 6.0, -0.0, -0.5, -1.0, -1.5, -2.0, -3.0, -4.0, -6.0])


def pack_weight(w, fmt):
    k, n = w.shape
    w = f64(np.asarray(w, np.float32).astype(ml_dtypes.bfloat16)).reshape(k // 32, 32, n)
    amax = np.abs(w).max(1)
    if fmt == "e4m3":
        byte = np.frexp(amax)[1] - 1 + 127 - 7
    else:
        mant, ex = np.frexp(amax / 6.0)
        byte = np.where(mant > 0.5, ex, ex - 1) + 127
    byte = np.clip(np.where(amax > 0, byte, 1), 1, 254)
    scaled = (w * np.exp2(127.0 - byte)[:, None, :]).reshape(k, n).astype(np.float32)
    by_word = np.ascontiguousarray(scaled.reshape(k // 512, 128, 4, n).transpose(0, 1, 3, 2))
    if fmt == "e4m3":
        words = by_word.astype(ml_dtypes.float8_e4m3fn).view(np.uint8)
    else:
        c = by_word.astype(ml_dtypes.float4_e2m1fn).view(np.uint8) & 0xF
        words = (c[..., 0::2] | (c[..., 1::2] << 4)).reshape(k // 512, 128, 2 * n)
    return np.ascontiguousarray(words), np.ascontiguousarray(byte.astype(np.uint8).reshape(k // 512, 16, n))


def unpack_weight(words, scales, fmt):
    g, _, n = scales.shape
    words = np.ascontiguousarray(words).reshape(g, 128, n, -1)
    if fmt == "e4m3":
        vals = words.view(ml_dtypes.float8_e4m3fn).astype(np.float64)
    else:
        nib = np.empty((g, 128, n, 4), np.uint8)
        nib[..., 0::2] = words & 0xF
        nib[..., 1::2] = words >> 4
        vals = E2M1[nib]
    vals = vals * np.repeat(np.exp2(scales.astype(np.float64) - 127.0), 8, axis=1)[..., None]
    return vals.transpose(0, 1, 3, 2).reshape(g * 512, n)


def gelu(v):
    return 0.5 * v * (1.0 + np.tanh(np.sqrt(2.0 / np.pi) * (v + 0.044715 * v**3)))


def twice(P):
    return np.random.permutation(np.repeat(np.arange(P), 2))


K, H, T, S, P = 1536, 1024, 4096, 1024, 512


def setup_inputs():
    n = np.random.standard_normal
    s = mx_kscale(K)[:, None]
    u = mx_kscale(H)[:, None]
    d = {}
    d["tab_words"], d["tab_scales"] = pack_weight(n((K, T)) * s, "e4m3")
    d["w1"] = (n((K, H)) / K ** 0.5 / s * u.T).astype(np.float32)
    d["w2"] = (1.2 * n((H, H)) / H ** 0.5 / u).astype(np.float32)
    d["w4_words"], d["w4_scales"] = pack_weight(-1.2 * n((H, H)) / H ** 0.5 / u, "e2m1")
    d["field"] = np.exp(0.5 * n((H, P))).astype(np.float32)
    d["gain"] = (1.5 * np.exp(0.3 * n(H)) / u[:, 0]).astype(np.float32)
    d["offs"] = striped(np.random.permutation(T)[:S])
    d["pos1"] = striped(np.random.permutation(S)[:P])
    d["pos2"] = striped(np.random.permutation(S)[:P])
    d["pos3"] = striped(twice(P))
    return d


def reference(tab_words, tab_scales, w1, w2, w4_words, w4_scales, field, gain, offs, pos1, pos2, pos3):
    v = unpack_weight(tab_words, tab_scales, "e4m3")[:, unstriped(offs)]
    h = mxq(f64(w1), 0, "e4m3").T @ v
    lead = h[:, unstriped(pos1)]
    trail = h[:, unstriped(pos2)]
    high = np.maximum(lead, trail) * f64(field)
    low = np.minimum(lead, trail)
    w4 = unpack_weight(w4_words, w4_scales, "e2m1")
    y = mxq(f64(w2), 0, "e4m3").T @ mxq(high, 0, "e4m3") + w4.T @ mxq(low, 0, "e4m3")
    up = y[:, unstriped(pos3)]
    own = h * f64(gain)[:, None]
    return up / (1.0 + np.exp(-up)) - own / (1.0 + np.exp(-own))

@@ -1,0 +1,289 @@
+from contextlib import ExitStack
+
+import concourse.mybir as mybir
+
+K, H, T, S, J = 1536, 1024, 4096, 1024, 512
+FLOPS = 2 * K * H * S + 2 * 2 * H * H * J
+
+F32 = mybir.dt.float32
+BF16 = mybir.dt.bfloat16
+I32 = mybir.dt.int32
+U32 = mybir.dt.uint32
+U16 = mybir.dt.uint16
+U8 = mybir.dt.uint8
+FP8X4 = mybir.dt.float8_e4m3fn_x4
+FP4X4 = mybir.dt.float4_e2m1fn_x4
+ALU = mybir.AluOpType
+SILU = mybir.ActivationFunctionType.Silu
+
+P = 128
+PACK = 4
+PASS = P * PACK
+BANK = 512
+K_PASSES = K // PASS
+BLOCKS = H // PASS
+SLICES = BLOCKS * PACK
+Y_WINDOWS = 3
+
+
+def tile_list_blade_edge_damage_kernel(
+    tc, tab_words, tab_scales, w1, w2, w4_words, w4_scales, field, gain, offs, pos1, pos2, pos3, out
+):
+    nc = tc.nc
+    with ExitStack() as ctx:
+        lists = ctx.enter_context(tc.tile_pool(name="lists", bufs=1))
+        keep = ctx.enter_context(tc.tile_pool(name="keep", bufs=1))
+        big = ctx.enter_context(tc.tile_pool(name="big", bufs=3))
+        stage = ctx.enter_context(tc.tile_pool(name="stage", bufs=6))
+        rounded = ctx.enter_context(tc.tile_pool(name="rounded", bufs=4))
+        psum = ctx.enter_context(tc.psum_pool(name="psum", bufs=1))
+
+        banks = [psum.tile([P, BANK], F32, name=f"bank{i}") for i in range(8)]
+
+        offs_t = lists.tile([P, S // 16], U16, name="offs_t")
+        pos1_t = lists.tile([P, J // 16], U16, name="pos1_t")
+        pos2_t = lists.tile([P, J // 16], U16, name="pos2_t")
+        pos3_t = lists.tile([P, S // 16], U16, name="pos3_t")
+
+        tab_planes = keep.tile([P, T], U8, name="tab_planes", align_bytes=64)
+        nc.vector.memset(tab_planes[:].bitcast(I32), 0)
+        w4_planes_raw = keep.tile([P, BLOCKS, H], U8, name="w4_planes_raw", align_bytes=64)
+        nc.vector.memset(w4_planes_raw[:].rearrange("p a n -> p (a n)").bitcast(I32), 0)
+        y_win = [keep.tile([P, 2 * J], F32, name=f"y_win{i}") for i in range(Y_WINDOWS)]
+        for w in y_win:
+            nc.vector.memset(w[:, J:], 0.0)
+
+        def load_table(a):
+            words = big.tile([P, T], U32, name="tab_pass", tag="big", align_bytes=64)
+            nc.sync.dma_start(
+                out=words[:].bitcast(I32),
+                in_=tab_words[a].rearrange("p n i -> p (n i)").bitcast(I32),
+            )
+            return words
+
+        def load_weight(w, a, b, parts):
+            width = PASS // parts
+            raws = []
+            for c in range(parts):
+                raw = stage.tile([P, PACK, width], F32, name="w_raw", tag="stage", align_bytes=64)
+                c0 = b * PASS + c * width
+                nc.sync.dma_start(
+                    out=raw[:],
+                    in_=w[a * PASS : (a + 1) * PASS, c0 : c0 + width].rearrange("(p j) c -> p j c", j=PACK),
+                )
+                raws.append(raw)
+            return raws
+
+        def round_weight(raws, copies):
+            grouped = rounded.tile([P, PACK * PASS], BF16, name="grouped", tag="rounded", align_bytes=64)
+            dealt = grouped[:].rearrange("p (t m j) -> p m j t", t=PACK, j=PACK)
+            share = P // len(raws)
+            for c, raw in enumerate(raws):
+                copies[c](
+                    out=dealt[:, c * share : (c + 1) * share, :, :],
+                    in_=raw[:].rearrange("p j (m t) -> p m j t", t=PACK),
+                )
+            return grouped
+
+        def quantize(grouped, name):
+            codes = keep.tile([P, PASS], U32, name=name + "_codes", align_bytes=64)
+            plane = keep.tile([P, PASS], U8, name=name + "_plane", align_bytes=64)
+            nc.vector.quantize_mx(out=codes[:].bitcast(FP8X4), scales=plane[:], in_=grouped[:])
+            return codes, plane
+
+        nc.sync.dma_start(offs_t[:], offs)
+        tab0 = load_table(0)
+        for q in range(4):
+            nc.sync.dma_start(
+                out=tab_planes[32 * q : 32 * q + 4 * K_PASSES, :].bitcast(I32),
+                in_=tab_scales[:, 4 * q : 4 * q + 4, :].bitcast(I32),
+            )
+        nc.sync.dma_start(pos1_t[:], pos1)
+        nc.sync.dma_start(pos2_t[:], pos2)
+        w1_raw = {(0, 0): load_weight(w1, 0, 0, 1)}
+        tab1 = load_table(1)
+        w1_raw[1, 0] = load_weight(w1, 1, 0, 1)
+        tab2 = load_table(2)
+        w1_raw[2, 0] = load_weight(w1, 2, 0, 2)
+        w4_raw = stage.tile([P, BLOCKS, 2 * H], U8, name="w4_raw", tag="stage", align_bytes=64)
+        nc.sync.dma_start(
+            out=w4_raw[:].bitcast(I32), in_=w4_words.rearrange("a p n -> p a n").bitcast(I32)
+        )
+        for q in range(4):
+            nc.sync.dma_start(
+                out=w4_planes_raw[32 * q : 32 * q + 4, :, :].bitcast(I32),
+                in_=w4_scales[:, 4 * q : 4 * q + 4, :].rearrange("a r n -> r a n").bitcast(I32),
+            )
+        gain_t = keep.tile([P, BLOCKS, PACK], F32, name="gain_t")
+        nc.sync.dma_start(out=gain_t[:], in_=gain.rearrange("(b p t) -> p b t", p=P, t=PACK))
+
+        picked = []
+        picked_planes = keep.tile([P, S], U8, name="picked_planes", align_bytes=64)
+        w1_q = {}
+        for a, words in enumerate((tab0, tab1, tab2)):
+            got = keep.tile([P, S], U32, name=f"picked{a}", align_bytes=64)
+            nc.vector.tensor_copy(got[:], words[:].indirect(offs_t[:]))
+            picked.append(got)
+            if a == 0:
+                nc.vector.tensor_copy(picked_planes[:], tab_planes[:].indirect(offs_t[:]))
+            copies = [nc.scalar.copy, nc.vector.tensor_copy]
+            w1_q[a, 0] = quantize(round_weight(w1_raw[a, 0], copies), f"w1_{a}0")
+
+        def h_pass(a, b, t, half):
+            codes, plane = w1_q[a, b]
+            rows = slice(t * P, (t + 1) * P)
+            cols = slice(half * BANK, (half + 1) * BANK)
+            nc.tensor.matmul_mx(
+                out=banks[2 * t + half][:],
+                lhsT=codes[:, rows].bitcast(FP8X4),
+                lhsT_scale=plane[:, rows],
+                rhs=picked[a][:, cols].bitcast(FP8X4),
+                rhs_scale=picked_planes[4 * a : P, cols],
+                start=(a == 0),
+                stop=(a == K_PASSES - 1),
+            )
+
+        h = [keep.tile([P, S], F32, name=f"h{s}") for s in range(SLICES)]
+
+        def h_out(b, t):
+            for half in range(2):
+                nc.scalar.copy(
+                    out=h[PACK * b + t][:, half * BANK : (half + 1) * BANK], in_=banks[2 * t + half][:]
+                )
+
+        for a in range(K_PASSES):
+            for t in range(PACK):
+                for half in range(2):
+                    h_pass(a, 0, t, half)
+                if a == K_PASSES - 1:
+                    h_out(0, t)
+
+        w4_codes = keep.tile([P, BLOCKS * 2 * H], U8, name="w4_codes", align_bytes=64)
+        nc.vector.tensor_copy(
+            out=w4_codes[:].bitcast(U16).rearrange("p (g t q) -> p g q t", t=PACK, q=P),
+            in_=w4_raw[:].rearrange("p a n -> p (a n)").bitcast(U16).rearrange("p (g q t) -> p g q t", t=PACK, q=P),
+        )
+        w4_planes = keep.tile([P, BLOCKS * H], U8, name="w4_planes", align_bytes=64)
+        nc.vector.tensor_copy(
+            out=w4_planes[:].rearrange("p (g t q) -> p g q t", t=PACK, q=P),
+            in_=w4_planes_raw[:].rearrange("p a (b q t) -> p (a b) q t", t=PACK, q=P),
+        )
+
+        for a in range(K_PASSES):
+            w1_raw[a, 1] = load_weight(w1, a, 1, 1)
+        field_t = []
+        for b in range(BLOCKS):
+            field_t.append(keep.tile([P, PACK, J], F32, name=f"field{b}"))
+
+        def load_field(b):
+            nc.sync.dma_start(
+                out=field_t[b][:], in_=field[b * PASS : (b + 1) * PASS, :].rearrange("(p t) j -> p t j", t=PACK)
+            )
+
+        load_field(0)
+        w2_raw = {}
+        for a in range(BLOCKS):
+            w2_raw[a, 0] = load_weight(w2, a, 0, 1)
+        load_field(1)
+        nc.sync.dma_start(pos3_t[:], pos3)
+        for a in range(BLOCKS):
+            w2_raw[a, 1] = load_weight(w2, a, 1, 1)
+
+        def pick_pair(pair, b, t):
+            window = h[PACK * b + t]
+            nc.vector.tensor_copy(pair[:, 0, t, :], window[:].indirect(pos1_t[:]))
+            nc.vector.tensor_copy(pair[:, 1, t, :], window[:].indirect(pos2_t[:]))
+
+        def join(pair, b):
+            woven = "p t (c i) -> p c t i"
+            larger = big.tile([P, PACK, J], F32, name="larger", tag="big", align_bytes=64)
+            low = rounded.tile([P, PACK * J], BF16, name="low", tag="rounded", align_bytes=64)
+            high = rounded.tile([P, PACK * J], BF16, name="high", tag="rounded", align_bytes=64)
+            nc.vector.tensor_tensor(
+                out=low[:].rearrange("p (c i t) -> p c t i", i=4, t=PACK),
+                in0=pair[:, 0, :, :].rearrange(woven, i=4),
+                in1=pair[:, 1, :, :].rearrange(woven, i=4),
+                op=ALU.min,
+            )
+            nc.vector.tensor_tensor(out=larger[:], in0=pair[:, 0, :, :], in1=pair[:, 1, :, :], op=ALU.max)
+            low_q = quantize(low, f"low{b}")
+            nc.vector.tensor_tensor(
+                out=high[:].rearrange("p (c i t) -> p c t i", i=4, t=PACK),
+                in0=larger[:].rearrange(woven, i=4),
+                in1=field_t[b][:].rearrange(woven, i=4),
+                op=ALU.mult,
+            )
+            return low_q, quantize(high, f"high{b}")
+
+        pair0 = big.tile([P, 2, PACK, J], F32, name="pair0", tag="big", align_bytes=64)
+        for t in range(PACK):
+            pick_pair(pair0, 0, t)
+            if t < K_PASSES:
+                w1_q[t, 1] = quantize(round_weight(w1_raw[t, 1], [nc.scalar.copy]), f"w1_{t}1")
+        for t in range(PACK):
+            for half in range(2):
+                for a in range(K_PASSES):
+                    h_pass(a, 1, t, half)
+            h_out(1, t)
+        joined = [join(pair0, 0)]
+
+        pair1 = big.tile([P, 2, PACK, J], F32, name="pair1", tag="big", align_bytes=64)
+        w2_q = {}
+        for t in range(PACK):
+            pick_pair(pair1, 1, t)
+            a, b = t % BLOCKS, t // BLOCKS
+            w2_q[a, b] = quantize(round_weight(w2_raw[a, b], [nc.scalar.copy]), f"w2_{a}{b}")
+
+        def y_low(a, s, start):
+            codes, plane = joined[a][0]
+            c0 = a * H + s * P
+            nc.tensor.matmul_mx(
+                out=banks[s][:],
+                lhsT=w4_codes[:, 2 * c0 : 2 * (c0 + P)].bitcast(FP4X4),
+                lhsT_scale=w4_planes[:, c0 : c0 + P],
+                rhs=codes[:].bitcast(FP8X4),
+                rhs_scale=plane[:],
+                start=start,
+                stop=False,
+            )
+
+        def y_high(a, s, stop):
+            codes, plane = joined[a][1]
+            w_codes, w_plane = w2_q[a, s // PACK]
+            rows = slice((s % PACK) * P, (s % PACK + 1) * P)
+            nc.tensor.matmul_mx(
+                out=banks[s][:],
+                lhsT=w_codes[:, rows].bitcast(FP8X4),
+                lhsT_scale=w_plane[:, rows],
+                rhs=codes[:].bitcast(FP8X4),
+                rhs_scale=plane[:],
+                start=False,
+                stop=stop,
+            )
+
+        for s in range(SLICES):
+            y_low(0, s, True)
+            y_high(0, s, False)
+        joined.append(join(pair1, 1))
+        for s in range(SLICES):
+            nc.scalar.activation(
+                out=h[s][:], in_=h[s][:], func=SILU, scale=gain_t[:, s // PACK, s % PACK : s % PACK + 1]
+            )
+        for s in range(SLICES):
+            y_low(1, s, False)
+        for s in range(SLICES):
+            b, t = divmod(s, PACK)
+            y_high(1, s, True)
+            window = y_win[s % Y_WINDOWS]
+            nc.scalar.activation(out=window[:, :J], in_=banks[s][:], func=SILU)
+            rows = out[b * PASS : (b + 1) * PASS, :].rearrange("(p t) m -> p t m", t=PACK)
+            result = stage.tile([P, S], F32, name="result", tag="stage", align_bytes=64)
+            for half in range(2):
+                cols = slice(half * J, (half + 1) * J)
+                nc.vector.tensor_tensor(
+                    out=result[:, cols],
+                    in0=window[:].indirect(pos3_t[:, half * (J // 16) : (half + 1) * (J // 16)]),
+                    in1=h[s][:, cols],
+                    op=ALU.subtract,
+                )
+            nc.sync.dma_start(out=rows[:, t, :], in_=result[:])

@@ -23,7 +23,7 @@ BANK = 512
 K_PASSES = K // PASS
 BLOCKS = H // PASS
 SLICES = BLOCKS * PACK
-Y_WINDOWS = 3
+Y_WINDOWS = 2
 
 
 def tile_list_blade_edge_damage_kernel(
@@ -36,6 +36,7 @@ def tile_list_blade_edge_damage_kernel(
         big = ctx.enter_context(tc.tile_pool(name="big", bufs=3))
         stage = ctx.enter_context(tc.tile_pool(name="stage", bufs=6))
         rounded = ctx.enter_context(tc.tile_pool(name="rounded", bufs=4))
+        turn = ctx.enter_context(tc.tile_pool(name="turn", bufs=1))
         psum = ctx.enter_context(tc.psum_pool(name="psum", bufs=1))
 
         banks = [psum.tile([P, BANK], F32, name=f"bank{i}") for i in range(8)]
@@ -49,6 +50,16 @@ def tile_list_blade_edge_damage_kernel(
         nc.vector.memset(tab_planes[:].bitcast(I32), 0)
         w4_planes_raw = keep.tile([P, BLOCKS, H], U8, name="w4_planes_raw", align_bytes=64)
         nc.vector.memset(w4_planes_raw[:].rearrange("p a n -> p (a n)").bitcast(I32), 0)
+        for q in range(4):
+            nc.gpsimd.dma_start(
+                out=tab_planes[32 * q : 32 * q + 4 * K_PASSES, :].bitcast(I32),
+                in_=tab_scales[:, 4 * q : 4 * q + 4, :].bitcast(I32),
+            )
+        for q in range(4):
+            nc.gpsimd.dma_start(
+                out=w4_planes_raw[32 * q : 32 * q + 4, :, :].bitcast(I32),
+                in_=w4_scales[:, 4 * q : 4 * q + 4, :].rearrange("a r n -> r a n").bitcast(I32),
+            )
         y_win = [keep.tile([P, 2 * J], F32, name=f"y_win{i}") for i in range(Y_WINDOWS)]
         for w in y_win:
             nc.vector.memset(w[:, J:], 0.0)
@@ -74,8 +85,8 @@ def tile_list_blade_edge_damage_kernel(
                 raws.append(raw)
             return raws
 
-        def round_weight(raws, copies):
-            grouped = rounded.tile([P, PACK * PASS], BF16, name="grouped", tag="rounded", align_bytes=64)
+        def round_weight(raws, copies, pool=rounded):
+            grouped = pool.tile([P, PACK * PASS], BF16, name="grouped", tag="rounded", align_bytes=64)
             dealt = grouped[:].rearrange("p (t m j) -> p m j t", t=PACK, j=PACK)
             share = P // len(raws)
             for c, raw in enumerate(raws):
@@ -85,19 +96,18 @@ def tile_list_blade_edge_damage_kernel(
                 )
             return grouped
 
-        def quantize(grouped, name):
-            codes = keep.tile([P, PASS], U32, name=name + "_codes", align_bytes=64)
+        def quantize(grouped, name, codes=None, cuts=(0, PASS)):
+            if codes is None:
+                codes = keep.tile([P, PASS], U32, name=name + "_codes", align_bytes=64)
             plane = keep.tile([P, PASS], U8, name=name + "_plane", align_bytes=64)
-            nc.vector.quantize_mx(out=codes[:].bitcast(FP8X4), scales=plane[:], in_=grouped[:])
+            for c0, c1 in zip(cuts, cuts[1:]):
+                nc.vector.quantize_mx(
+                    out=codes[:, c0:c1].bitcast(FP8X4), scales=plane[:, c0:c1], in_=grouped[:, PACK * c0 : PACK * c1]
+                )
             return codes, plane
 
         nc.sync.dma_start(offs_t[:], offs)
         tab0 = load_table(0)
-        for q in range(4):
-            nc.sync.dma_start(
-                out=tab_planes[32 * q : 32 * q + 4 * K_PASSES, :].bitcast(I32),
-                in_=tab_scales[:, 4 * q : 4 * q + 4, :].bitcast(I32),
-            )
         nc.sync.dma_start(pos1_t[:], pos1)
         nc.sync.dma_start(pos2_t[:], pos2)
         w1_raw = {(0, 0): load_weight(w1, 0, 0, 1)}
@@ -109,11 +119,6 @@ def tile_list_blade_edge_damage_kernel(
         nc.sync.dma_start(
             out=w4_raw[:].bitcast(I32), in_=w4_words.rearrange("a p n -> p a n").bitcast(I32)
         )
-        for q in range(4):
-            nc.sync.dma_start(
-                out=w4_planes_raw[32 * q : 32 * q + 4, :, :].bitcast(I32),
-                in_=w4_scales[:, 4 * q : 4 * q + 4, :].rearrange("a r n -> r a n").bitcast(I32),
-            )
         gain_t = keep.tile([P, BLOCKS, PACK], F32, name="gain_t")
         nc.sync.dma_start(out=gain_t[:], in_=gain.rearrange("(b p t) -> p b t", p=P, t=PACK))
 
@@ -127,7 +132,8 @@ def tile_list_blade_edge_damage_kernel(
             if a == 0:
                 nc.vector.tensor_copy(picked_planes[:], tab_planes[:].indirect(offs_t[:]))
             copies = [nc.scalar.copy, nc.vector.tensor_copy]
-            w1_q[a, 0] = quantize(round_weight(w1_raw[a, 0], copies), f"w1_{a}0")
+            cuts = (0, P, 2 * P, PASS) if a == K_PASSES - 1 else (0, PASS)
+            w1_q[a, 0] = quantize(round_weight(w1_raw[a, 0], copies), f"w1_{a}0", cuts=cuts)
 
         def h_pass(a, b, t, half):
             codes, plane = w1_q[a, b]
@@ -198,7 +204,7 @@ def tile_list_blade_edge_damage_kernel(
             woven = "p t (c i) -> p c t i"
             larger = big.tile([P, PACK, J], F32, name="larger", tag="big", align_bytes=64)
             low = rounded.tile([P, PACK * J], BF16, name="low", tag="rounded", align_bytes=64)
-            high = rounded.tile([P, PACK * J], BF16, name="high", tag="rounded", align_bytes=64)
+            high = turn.tile([P, PACK * J], BF16, name="high", tag="rounded", align_bytes=64)
             nc.vector.tensor_tensor(
                 out=low[:].rearrange("p (c i t) -> p c t i", i=4, t=PACK),
                 in0=pair[:, 0, :, :].rearrange(woven, i=4),
@@ -219,7 +225,9 @@ def tile_list_blade_edge_damage_kernel(
         for t in range(PACK):
             pick_pair(pair0, 0, t)
             if t < K_PASSES:
-                w1_q[t, 1] = quantize(round_weight(w1_raw[t, 1], [nc.scalar.copy]), f"w1_{t}1")
+                w1_q[t, 1] = quantize(
+                    round_weight(w1_raw[t, 1], [nc.scalar.copy], turn if t == K_PASSES - 1 else rounded), f"w1_{t}1"
+                )
         for t in range(PACK):
             for half in range(2):
                 for a in range(K_PASSES):
@@ -231,8 +239,8 @@ def tile_list_blade_edge_damage_kernel(
         w2_q = {}
         for t in range(PACK):
             pick_pair(pair1, 1, t)
-            a, b = t % BLOCKS, t // BLOCKS
-            w2_q[a, b] = quantize(round_weight(w2_raw[a, b], [nc.scalar.copy]), f"w2_{a}{b}")
+            if t < BLOCKS:
+                w2_q[t, 0] = quantize(round_weight(w2_raw[t, 0], [nc.scalar.copy]), f"w2_{t}0")
 
         def y_low(a, s, start):
             codes, plane = joined[a][0]
@@ -263,8 +271,12 @@ def tile_list_blade_edge_damage_kernel(
 
         for s in range(SLICES):
             y_low(0, s, True)
-            y_high(0, s, False)
+            if s < PACK:
+                y_high(0, s, False)
         joined.append(join(pair1, 1))
+        late_codes = turn.tile([P, BLOCKS, PASS], U32, name="late_codes", tag="rounded", align_bytes=64)
+        for a in range(BLOCKS):
+            w2_q[a, 1] = quantize(round_weight(w2_raw[a, 1], [nc.scalar.copy]), f"w2_{a}1", late_codes[:, a, :])
         for s in range(SLICES):
             nc.scalar.activation(
                 out=h[s][:], in_=h[s][:], func=SILU, scale=gain_t[:, s // PACK, s % PACK : s % PACK + 1]
@@ -273,6 +285,8 @@ def tile_list_blade_edge_damage_kernel(
             y_low(1, s, False)
         for s in range(SLICES):
             b, t = divmod(s, PACK)
+            if s >= PACK:
+                y_high(0, s, False)
             y_high(1, s, True)
             window = y_win[s % Y_WINDOWS]
             nc.scalar.activation(out=window[:, :J], in_=banks[s][:], func=SILU)
@@ -286,4 +300,7 @@ def tile_list_blade_edge_damage_kernel(
                     in1=h[s][:, cols],
                     op=ALU.subtract,
                 )
-            nc.sync.dma_start(out=rows[:, t, :], in_=result[:])
+                if s == SLICES - 1:
+                    nc.sync.dma_start(out=rows[:, t, cols], in_=result[:, cols])
+            if s < SLICES - 1:
+                nc.sync.dma_start(out=rows[:, t, :], in_=result[:])

@@ -34,9 +34,10 @@ def tile_list_blade_edge_damage_kernel(
         lists = ctx.enter_context(tc.tile_pool(name="lists", bufs=1))
         keep = ctx.enter_context(tc.tile_pool(name="keep", bufs=1))
         big = ctx.enter_context(tc.tile_pool(name="big", bufs=3))
-        stage = ctx.enter_context(tc.tile_pool(name="stage", bufs=6))
+        stage = ctx.enter_context(tc.tile_pool(name="stage", bufs=5))
         rounded = ctx.enter_context(tc.tile_pool(name="rounded", bufs=4))
         turn = ctx.enter_context(tc.tile_pool(name="turn", bufs=1))
+        wide = ctx.enter_context(tc.tile_pool(name="wide", bufs=1))
         psum = ctx.enter_context(tc.psum_pool(name="psum", bufs=1))
 
         banks = [psum.tile([P, BANK], F32, name=f"bank{i}") for i in range(8)]
@@ -202,9 +203,9 @@ def tile_list_blade_edge_damage_kernel(
 
         def join(pair, b):
             woven = "p t (c i) -> p c t i"
-            larger = big.tile([P, PACK, J], F32, name="larger", tag="big", align_bytes=64)
-            low = rounded.tile([P, PACK * J], BF16, name="low", tag="rounded", align_bytes=64)
-            high = turn.tile([P, PACK * J], BF16, name="high", tag="rounded", align_bytes=64)
+            larger = wide.tile([P, PACK, J], F32, name="larger", tag="rounded", align_bytes=64)
+            low = (rounded if b else turn).tile([P, PACK * J], BF16, name="low", tag="rounded", align_bytes=64)
+            high = (turn if b else rounded).tile([P, PACK * J], BF16, name="high", tag="rounded", align_bytes=64)
             nc.vector.tensor_tensor(
                 out=low[:].rearrange("p (c i t) -> p c t i", i=4, t=PACK),
                 in0=pair[:, 0, :, :].rearrange(woven, i=4),
@@ -213,20 +214,22 @@ def tile_list_blade_edge_damage_kernel(
             )
             nc.vector.tensor_tensor(out=larger[:], in0=pair[:, 0, :, :], in1=pair[:, 1, :, :], op=ALU.max)
             low_q = quantize(low, f"low{b}")
-            nc.vector.tensor_tensor(
-                out=high[:].rearrange("p (c i t) -> p c t i", i=4, t=PACK),
-                in0=larger[:].rearrange(woven, i=4),
-                in1=field_t[b][:].rearrange(woven, i=4),
-                op=ALU.mult,
-            )
-            return low_q, quantize(high, f"high{b}")
+            cuts = (0, J // 2, J) if b else (0, J)
+            for c0, c1 in zip(cuts, cuts[1:]):
+                nc.vector.tensor_tensor(
+                    out=high[:, PACK * c0 : PACK * c1].rearrange("p (c i t) -> p c t i", i=4, t=PACK),
+                    in0=larger[:, :, c0:c1].rearrange(woven, i=4),
+                    in1=field_t[b][:, :, c0:c1].rearrange(woven, i=4),
+                    op=ALU.mult,
+                )
+            return low_q, quantize(high, f"high{b}", cuts=cuts)
 
         pair0 = big.tile([P, 2, PACK, J], F32, name="pair0", tag="big", align_bytes=64)
         for t in range(PACK):
             pick_pair(pair0, 0, t)
             if t < K_PASSES:
                 w1_q[t, 1] = quantize(
-                    round_weight(w1_raw[t, 1], [nc.scalar.copy], turn if t == K_PASSES - 1 else rounded), f"w1_{t}1"
+                    round_weight(w1_raw[t, 1], [nc.scalar.copy], (rounded, wide, turn)[t]), f"w1_{t}1"
                 )
         for t in range(PACK):
             for half in range(2):
@@ -292,11 +295,12 @@ def tile_list_blade_edge_damage_kernel(
             nc.scalar.activation(out=window[:, :J], in_=banks[s][:], func=SILU)
             rows = out[b * PASS : (b + 1) * PASS, :].rearrange("(p t) m -> p t m", t=PACK)
             result = stage.tile([P, S], F32, name="result", tag="stage", align_bytes=64)
-            for half in range(2):
-                cols = slice(half * J, (half + 1) * J)
+            cuts = (0, J, J + J // 2, S) if s == SLICES - 1 else (0, J, S)
+            for c0, c1 in zip(cuts, cuts[1:]):
+                cols = slice(c0, c1)
                 nc.vector.tensor_tensor(
                     out=result[:, cols],
-                    in0=window[:].indirect(pos3_t[:, half * (J // 16) : (half + 1) * (J // 16)]),
+                    in0=window[:].indirect(pos3_t[:, c0 // 16 : c1 // 16]),
                     in1=h[s][:, cols],
                     op=ALU.subtract,
                 )

from contextlib import ExitStack

import concourse.mybir as mybir

K, H, T, S, J = 1536, 1024, 4096, 1024, 512
FLOPS = 2 * K * H * S + 2 * 2 * H * H * J

F32 = mybir.dt.float32
BF16 = mybir.dt.bfloat16
I32 = mybir.dt.int32
U32 = mybir.dt.uint32
U16 = mybir.dt.uint16
U8 = mybir.dt.uint8
FP8X4 = mybir.dt.float8_e4m3fn_x4
FP4X4 = mybir.dt.float4_e2m1fn_x4
ALU = mybir.AluOpType
SILU = mybir.ActivationFunctionType.Silu

P = 128
PACK = 4
PASS = P * PACK
BANK = 512
K_PASSES = K // PASS
BLOCKS = H // PASS
SLICES = BLOCKS * PACK
Y_WINDOWS = 2


def tile_list_blade_edge_damage_kernel(
    tc, tab_words, tab_scales, w1, w2, w4_words, w4_scales, field, gain, offs, pos1, pos2, pos3, out
):
    nc = tc.nc
    with ExitStack() as ctx:
        lists = ctx.enter_context(tc.tile_pool(name="lists", bufs=1))
        keep = ctx.enter_context(tc.tile_pool(name="keep", bufs=1))
        big = ctx.enter_context(tc.tile_pool(name="big", bufs=3))
        stage = ctx.enter_context(tc.tile_pool(name="stage", bufs=5))
        rounded = ctx.enter_context(tc.tile_pool(name="rounded", bufs=4))
        turn = ctx.enter_context(tc.tile_pool(name="turn", bufs=1))
        wide = ctx.enter_context(tc.tile_pool(name="wide", bufs=1))
        psum = ctx.enter_context(tc.psum_pool(name="psum", bufs=1))

        banks = [psum.tile([P, BANK], F32, name=f"bank{i}") for i in range(8)]

        offs_t = lists.tile([P, S // 16], U16, name="offs_t")
        pos1_t = lists.tile([P, J // 16], U16, name="pos1_t")
        pos2_t = lists.tile([P, J // 16], U16, name="pos2_t")
        pos3_t = lists.tile([P, S // 16], U16, name="pos3_t")

        tab_planes = keep.tile([P, T], U8, name="tab_planes", align_bytes=64)
        nc.vector.memset(tab_planes[:].bitcast(I32), 0)
        w4_planes_raw = keep.tile([P, BLOCKS, H], U8, name="w4_planes_raw", align_bytes=64)
        nc.vector.memset(w4_planes_raw[:].rearrange("p a n -> p (a n)").bitcast(I32), 0)
        for q in range(4):
            nc.gpsimd.dma_start(
                out=tab_planes[32 * q : 32 * q + 4 * K_PASSES, :].bitcast(I32),
                in_=tab_scales[:, 4 * q : 4 * q + 4, :].bitcast(I32),
            )
        for q in range(4):
            nc.gpsimd.dma_start(
                out=w4_planes_raw[32 * q : 32 * q + 4, :, :].bitcast(I32),
                in_=w4_scales[:, 4 * q : 4 * q + 4, :].rearrange("a r n -> r a n").bitcast(I32),
            )
        y_win = [keep.tile([P, 2 * J], F32, name=f"y_win{i}") for i in range(Y_WINDOWS)]
        for w in y_win:
            nc.vector.memset(w[:, J:], 0.0)

        def load_table(a):
            words = big.tile([P, T], U32, name="tab_pass", tag="big", align_bytes=64)
            nc.sync.dma_start(
                out=words[:].bitcast(I32),
                in_=tab_words[a].rearrange("p n i -> p (n i)").bitcast(I32),
            )
            return words

        def load_weight(w, a, b, parts):
            width = PASS // parts
            raws = []
            for c in range(parts):
                raw = stage.tile([P, PACK, width], F32, name="w_raw", tag="stage", align_bytes=64)
                c0 = b * PASS + c * width
                nc.sync.dma_start(
                    out=raw[:],
                    in_=w[a * PASS : (a + 1) * PASS, c0 : c0 + width].rearrange("(p j) c -> p j c", j=PACK),
                )
                raws.append(raw)
            return raws

        def round_weight(raws, copies, pool=rounded):
            grouped = pool.tile([P, PACK * PASS], BF16, name="grouped", tag="rounded", align_bytes=64)
            dealt = grouped[:].rearrange("p (t m j) -> p m j t", t=PACK, j=PACK)
            share = P // len(raws)
            for c, raw in enumerate(raws):
                copies[c](
                    out=dealt[:, c * share : (c + 1) * share, :, :],
                    in_=raw[:].rearrange("p j (m t) -> p m j t", t=PACK),
                )
            return grouped

        def quantize(grouped, name, codes=None, cuts=(0, PASS)):
            if codes is None:
                codes = keep.tile([P, PASS], U32, name=name + "_codes", align_bytes=64)
            plane = keep.tile([P, PASS], U8, name=name + "_plane", align_bytes=64)
            for c0, c1 in zip(cuts, cuts[1:]):
                nc.vector.quantize_mx(
                    out=codes[:, c0:c1].bitcast(FP8X4), scales=plane[:, c0:c1], in_=grouped[:, PACK * c0 : PACK * c1]
                )
            return codes, plane

        nc.sync.dma_start(offs_t[:], offs)
        tab0 = load_table(0)
        nc.sync.dma_start(pos1_t[:], pos1)
        nc.sync.dma_start(pos2_t[:], pos2)
        w1_raw = {(0, 0): load_weight(w1, 0, 0, 1)}
        tab1 = load_table(1)
        w1_raw[1, 0] = load_weight(w1, 1, 0, 1)
        tab2 = load_table(2)
        w1_raw[2, 0] = load_weight(w1, 2, 0, 2)
        w4_raw = stage.tile([P, BLOCKS, 2 * H], U8, name="w4_raw", tag="stage", align_bytes=64)
        nc.sync.dma_start(
            out=w4_raw[:].bitcast(I32), in_=w4_words.rearrange("a p n -> p a n").bitcast(I32)
        )
        gain_t = keep.tile([P, BLOCKS, PACK], F32, name="gain_t")
        nc.sync.dma_start(out=gain_t[:], in_=gain.rearrange("(b p t) -> p b t", p=P, t=PACK))

        picked = []
        picked_planes = keep.tile([P, S], U8, name="picked_planes", align_bytes=64)
        w1_q = {}
        for a, words in enumerate((tab0, tab1, tab2)):
            got = keep.tile([P, S], U32, name=f"picked{a}", align_bytes=64)
            nc.vector.tensor_copy(got[:], words[:].indirect(offs_t[:]))
            picked.append(got)
            if a == 0:
                nc.vector.tensor_copy(picked_planes[:], tab_planes[:].indirect(offs_t[:]))
            copies = [nc.scalar.copy, nc.vector.tensor_copy]
            cuts = (0, P, 2 * P, PASS) if a == K_PASSES - 1 else (0, PASS)
            w1_q[a, 0] = quantize(round_weight(w1_raw[a, 0], copies), f"w1_{a}0", cuts=cuts)

        def h_pass(a, b, t, half):
            codes, plane = w1_q[a, b]
            rows = slice(t * P, (t + 1) * P)
            cols = slice(half * BANK, (half + 1) * BANK)
            nc.tensor.matmul_mx(
                out=banks[2 * t + half][:],
                lhsT=codes[:, rows].bitcast(FP8X4),
                lhsT_scale=plane[:, rows],
                rhs=picked[a][:, cols].bitcast(FP8X4),
                rhs_scale=picked_planes[4 * a : P, cols],
                start=(a == 0),
                stop=(a == K_PASSES - 1),
            )

        h = [keep.tile([P, S], F32, name=f"h{s}") for s in range(SLICES)]

        def h_out(b, t):
            for half in range(2):
                nc.scalar.copy(
                    out=h[PACK * b + t][:, half * BANK : (half + 1) * BANK], in_=banks[2 * t + half][:]
                )

        for a in range(K_PASSES):
            for t in range(PACK):
                for half in range(2):
                    h_pass(a, 0, t, half)
                if a == K_PASSES - 1:
                    h_out(0, t)

        w4_codes = keep.tile([P, BLOCKS * 2 * H], U8, name="w4_codes", align_bytes=64)
        nc.vector.tensor_copy(
            out=w4_codes[:].bitcast(U16).rearrange("p (g t q) -> p g q t", t=PACK, q=P),
            in_=w4_raw[:].rearrange("p a n -> p (a n)").bitcast(U16).rearrange("p (g q t) -> p g q t", t=PACK, q=P),
        )
        w4_planes = keep.tile([P, BLOCKS * H], U8, name="w4_planes", align_bytes=64)
        nc.vector.tensor_copy(
            out=w4_planes[:].rearrange("p (g t q) -> p g q t", t=PACK, q=P),
            in_=w4_planes_raw[:].rearrange("p a (b q t) -> p (a b) q t", t=PACK, q=P),
        )

        for a in range(K_PASSES):
            w1_raw[a, 1] = load_weight(w1, a, 1, 1)
        field_t = []
        for b in range(BLOCKS):
            field_t.append(keep.tile([P, PACK, J], F32, name=f"field{b}"))

        def load_field(b):
            nc.sync.dma_start(
                out=field_t[b][:], in_=field[b * PASS : (b + 1) * PASS, :].rearrange("(p t) j -> p t j", t=PACK)
            )

        load_field(0)
        w2_raw = {}
        for a in range(BLOCKS):
            w2_raw[a, 0] = load_weight(w2, a, 0, 1)
        load_field(1)
        nc.sync.dma_start(pos3_t[:], pos3)
        for a in range(BLOCKS):
            w2_raw[a, 1] = load_weight(w2, a, 1, 1)

        def pick_pair(pair, b, t):
            window = h[PACK * b + t]
            nc.vector.tensor_copy(pair[:, 0, t, :], window[:].indirect(pos1_t[:]))
            nc.vector.tensor_copy(pair[:, 1, t, :], window[:].indirect(pos2_t[:]))

        def join(pair, b):
            woven = "p t (c i) -> p c t i"
            larger = wide.tile([P, PACK, J], F32, name="larger", tag="rounded", align_bytes=64)
            low = (rounded if b else turn).tile([P, PACK * J], BF16, name="low", tag="rounded", align_bytes=64)
            high = (turn if b else rounded).tile([P, PACK * J], BF16, name="high", tag="rounded", align_bytes=64)
            nc.vector.tensor_tensor(
                out=low[:].rearrange("p (c i t) -> p c t i", i=4, t=PACK),
                in0=pair[:, 0, :, :].rearrange(woven, i=4),
                in1=pair[:, 1, :, :].rearrange(woven, i=4),
                op=ALU.min,
            )
            nc.vector.tensor_tensor(out=larger[:], in0=pair[:, 0, :, :], in1=pair[:, 1, :, :], op=ALU.max)
            low_q = quantize(low, f"low{b}")
            cuts = (0, J // 2, J) if b else (0, J)
            for c0, c1 in zip(cuts, cuts[1:]):
                nc.vector.tensor_tensor(
                    out=high[:, PACK * c0 : PACK * c1].rearrange("p (c i t) -> p c t i", i=4, t=PACK),
                    in0=larger[:, :, c0:c1].rearrange(woven, i=4),
                    in1=field_t[b][:, :, c0:c1].rearrange(woven, i=4),
                    op=ALU.mult,
                )
            return low_q, quantize(high, f"high{b}", cuts=cuts)

        pair0 = big.tile([P, 2, PACK, J], F32, name="pair0", tag="big", align_bytes=64)
        for t in range(PACK):
            pick_pair(pair0, 0, t)
            if t < K_PASSES:
                w1_q[t, 1] = quantize(
                    round_weight(w1_raw[t, 1], [nc.scalar.copy], (rounded, wide, turn)[t]), f"w1_{t}1"
                )
        for t in range(PACK):
            for half in range(2):
                for a in range(K_PASSES):
                    h_pass(a, 1, t, half)
            h_out(1, t)
        joined = [join(pair0, 0)]

        pair1 = big.tile([P, 2, PACK, J], F32, name="pair1", tag="big", align_bytes=64)
        w2_q = {}
        for t in range(PACK):
            pick_pair(pair1, 1, t)
            if t < BLOCKS:
                w2_q[t, 0] = quantize(round_weight(w2_raw[t, 0], [nc.scalar.copy]), f"w2_{t}0")

        def y_low(a, s, start):
            codes, plane = joined[a][0]
            c0 = a * H + s * P
            nc.tensor.matmul_mx(
                out=banks[s][:],
                lhsT=w4_codes[:, 2 * c0 : 2 * (c0 + P)].bitcast(FP4X4),
                lhsT_scale=w4_planes[:, c0 : c0 + P],
                rhs=codes[:].bitcast(FP8X4),
                rhs_scale=plane[:],
                start=start,
                stop=False,
            )

        def y_high(a, s, stop):
            codes, plane = joined[a][1]
            w_codes, w_plane = w2_q[a, s // PACK]
            rows = slice((s % PACK) * P, (s % PACK + 1) * P)
            nc.tensor.matmul_mx(
                out=banks[s][:],
                lhsT=w_codes[:, rows].bitcast(FP8X4),
                lhsT_scale=w_plane[:, rows],
                rhs=codes[:].bitcast(FP8X4),
                rhs_scale=plane[:],
                start=False,
                stop=stop,
            )

        for s in range(SLICES):
            y_low(0, s, True)
            if s < PACK:
                y_high(0, s, False)
        joined.append(join(pair1, 1))
        late_codes = turn.tile([P, BLOCKS, PASS], U32, name="late_codes", tag="rounded", align_bytes=64)
        for a in range(BLOCKS):
            w2_q[a, 1] = quantize(round_weight(w2_raw[a, 1], [nc.scalar.copy]), f"w2_{a}1", late_codes[:, a, :])
        for s in range(SLICES):
            nc.scalar.activation(
                out=h[s][:], in_=h[s][:], func=SILU, scale=gain_t[:, s // PACK, s % PACK : s % PACK + 1]
            )
        for s in range(SLICES):
            y_low(1, s, False)
        for s in range(SLICES):
            b, t = divmod(s, PACK)
            if s >= PACK:
                y_high(0, s, False)
            y_high(1, s, True)
            window = y_win[s % Y_WINDOWS]
            nc.scalar.activation(out=window[:, :J], in_=banks[s][:], func=SILU)
            rows = out[b * PASS : (b + 1) * PASS, :].rearrange("(p t) m -> p t m", t=PACK)
            result = stage.tile([P, S], F32, name="result", tag="stage", align_bytes=64)
            cuts = (0, J, J + J // 2, S) if s == SLICES - 1 else (0, J, S)
            for c0, c1 in zip(cuts, cuts[1:]):
                cols = slice(c0, c1)
                nc.vector.tensor_tensor(
                    out=result[:, cols],
                    in0=window[:].indirect(pos3_t[:, c0 // 16 : c1 // 16]),
                    in1=h[s][:, cols],
                    op=ALU.subtract,
                )
                if s == SLICES - 1:
                    nc.sync.dma_start(out=rows[:, t, cols], in_=result[:, cols])
            if s < SLICES - 1:
                nc.sync.dma_start(out=rows[:, t, :], in_=result[:])
